import numpy as np
import ml_dtypes


def mxq(x, axis, fmt="e4m3"):
    dtype, down = {"e4m3": (ml_dtypes.float8_e4m3fn, 7), "e5m2": (ml_dtypes.float8_e5m2, 14)}[fmt]
    v = np.moveaxis(np.asarray(x, np.float32).astype(ml_dtypes.bfloat16).astype(np.float64), axis, -1)
    blocks = v.reshape(v.shape[:-1] + (-1, 32))
    amax = np.abs(blocks).max(-1, keepdims=True)
    byte = np.maximum(np.where(amax > 0, np.frexp(amax)[1] - 1 + 127, 0) - down, 1)
    scale = np.exp2(byte - 127.0)
    codes = (blocks / scale).astype(np.float32).astype(dtype).astype(np.float64)
    return np.moveaxis((codes * scale).reshape(v.shape), -1, axis)


WIDE = False


def mx_kscale(k):
    if not WIDE:
        return np.ones(k)
    levels = np.array([10, -10, 5, -5, 0])
    if k % 512:
        return np.exp2(np.random.permutation(np.resize(levels, k // 32))).repeat(32)
    a = np.empty((k // 512, 16))
    for p in range(k // 512):
        a[p, :8] = np.random.permutation(np.resize(levels, 8))
        for g in range(8):
            far = levels[np.abs(levels - a[p, g]) >= 10]
            a[p, g + 8] = far[np.random.randint(len(far))]
    return np.exp2(a.ravel()).repeat(32)


def f64(x):
    return np.asarray(x).astype(np.float64)


def striped(idx):
    return np.tile(idx.reshape(-1, 16).T, (8, 1)).astype(np.uint16)


def unstriped(offs):
    return offs[:16].T.reshape(-1).astype(np.int64)


def pack_weight(w):
    k, n = w.shape
    w = f64(np.asarray(w, np.float32).astype(ml_dtypes.bfloat16)).reshape(k // 32, 32, n)
    amax = np.abs(w).max(1)
    byte = np.clip(np.where(amax > 0, np.frexp(amax)[1] - 1 + 127 - 7, 1), 1, 254)
    scaled = (w * np.exp2(127.0 - byte)[:, None, :]).reshape(k, n).astype(np.float32)
    words = np.ascontiguousarray(scaled.reshape(k // 512, 128, 4, n).transpose(0, 1, 3, 2)).astype(ml_dtypes.float8_e4m3fn).view(np.uint8)
    return words, np.ascontiguousarray(byte.astype(np.uint8).reshape(k // 512, 16, n))


def unpack_weight(words, scales):
    g, p, n, _ = words.shape
    vals = np.ascontiguousarray(words).view(ml_dtypes.float8_e4m3fn).astype(np.float64) * np.repeat(np.exp2(scales.astype(np.float64) - 127.0), 8, axis=1)[..., None]
    return vals.transpose(0, 1, 3, 2).reshape(g * 512, n)


E2M1 = np.array([0.0, 0.5, 1.0, 1.5, 2.0, 3.0, 4.0, 6.0, -0.0, -0.5, -1.0, -1.5, -2.0, -3.0, -4.0, -6.0])


def pack_fp4(w):
    k, n = w.shape
    w = f64(np.asarray(w, np.float32).astype(ml_dtypes.bfloat16)).reshape(k // 32, 32, n)
    amax = np.abs(w).max(1)
    mant, ex = np.frexp(amax / 6.0)
    byte = np.clip(np.where(amax > 0, np.where(mant > 0.5, ex, ex - 1) + 127, 1), 1, 254)
    scaled = (w * np.exp2(127.0 - byte)[:, None, :]).reshape(k, n).astype(np.float32)
    c = np.ascontiguousarray(scaled.reshape(k // 512, 128, 4, n).transpose(0, 1, 3, 2)).astype(ml_dtypes.float4_e2m1fn).view(np.uint8) & 0xF
    words = (c[..., 0::2] | (c[..., 1::2] << 4)).reshape(k // 512, 128, 2 * n)
    return np.ascontiguousarray(words), np.ascontiguousarray(byte.astype(np.uint8).reshape(k // 512, 16, n))


def unpack_fp4(words, scales):
    g, _, n = scales.shape
    words = np.ascontiguousarray(words).reshape(g, 128, n, 2)
    nib = np.empty((g, 128, n, 4), np.uint8)
    nib[..., 0::2] = words & 0xF
    nib[..., 1::2] = words >> 4
    vals = E2M1[nib] * np.repeat(np.exp2(scales.astype(np.float64) - 127.0), 8, axis=1)[..., None]
    return vals.transpose(0, 1, 3, 2).reshape(g * 512, n)


K, T, S, N, H = 1024, 2048, 512, 128, 512


def setup_inputs():
    n = np.random.standard_normal
    s = mx_kscale(K)[:, None]
    u = mx_kscale(H)
    packed_xT = pack_weight(n((K, T)) * s)
    packed_w1 = pack_fp4(n((K, H)) / np.sqrt(K) / s)
    packed_w2 = pack_fp4(n((K, H)) / np.sqrt(K) / s)
    packed_w3 = pack_fp4(n((H, N)) / np.sqrt(H) / u[:, None])
    return {
        "x_words": packed_xT[0],
        "x_scales": packed_xT[1],
        "w1_words": packed_w1[0],
        "w1_scales": packed_w1[1],
        "w2_words": packed_w2[0],
        "w2_scales": packed_w2[1],
        "eps": (np.random.uniform(0.3, 0.9, (H, 1))).astype(np.float32),
        "unit": (np.random.uniform(0.6, 1.4, (H, 1)) * u[:, None]).astype(np.float32),
        "w3_words": packed_w3[0],
        "w3_scales": packed_w3[1],
        "offs": striped(np.random.permutation(T)[:S]),
        "lft": striped(np.random.permutation(S)),
        "rgt": striped(np.random.permutation(S)),
    }


def reference(x_words, x_scales, w1_words, w1_scales, w2_words, w2_scales, eps, unit, w3_words, w3_scales, offs, lft, rgt):
    xq = unpack_weight(x_words, x_scales)[:, unstriped(offs)]
    vv = unpack_fp4(w1_words, w1_scales).T @ xq
    vb = np.tanh(vv)
    ww = unpack_fp4(w2_words, w2_scales).T @ xq
    vl = vb[:, unstriped(lft)]
    vr = vb[:, unstriped(rgt)]
    lap = vl + vr - (2.0 * vb)
    dv = vb - (0.6 * (vb * ((vb) ** 2))) - ww + 0.5 * lap
    vn = vb + 0.4 * dv
    wn = ww + 0.5 * (f64(eps) * vn - (0.6 * ww))
    vw = vn * wn
    hid = f64(unit) * (vw + vn[:, unstriped(rgt)])
    return unpack_fp4(w3_words, w3_scales).T @ mxq(hid, 0, "e4m3")

@@ -1,0 +1,221 @@
+import math
+from contextlib import ExitStack
+
+import concourse.mybir as mybir
+from concourse.masks import make_identity
+
+K, T, S, N, H = 1024, 2048, 512, 128, 512
+FLOPS = 2 * K * H * S * 2 + 2 * H * N * S
+
+F32 = mybir.dt.float32
+BF16 = mybir.dt.bfloat16
+I32 = mybir.dt.int32
+U32 = mybir.dt.uint32
+U16 = mybir.dt.uint16
+U8 = mybir.dt.uint8
+FP8X4 = mybir.dt.float8_e4m3fn_x4
+FP4X4 = mybir.dt.float4_e2m1fn_x4
+ACT = mybir.ActivationFunctionType
+ALU = mybir.AluOpType
+
+P = 128
+PASSES = K // 512
+TILES = H // P
+BLOCKS = S // P
+SPARE = 16
+HALF = S // 2
+FUSED = (0,)
+
+
+def tile_picked_yfhnag_mul_p_kernel(
+    tc, x_words, x_scales, w1_words, w1_scales, w2_words, w2_scales, eps, unit, w3_words, w3_scales, offs, lft, rgt, out
+):
+    nc = tc.nc
+    with ExitStack() as ctx:
+        keep = ctx.enter_context(tc.tile_pool(name="keep", bufs=1))
+        work = ctx.enter_context(tc.tile_pool(name="work", bufs=4))
+        psum = ctx.enter_context(tc.psum_pool(name="psum", bufs=1))
+
+        def load_planes(queue, plane, scales):
+            for q in range(4):
+                queue.dma_start(
+                    out=plane[32 * q : 32 * q + 4].bitcast(I32),
+                    in_=scales[:, 4 * q : 4 * q + 4, :].rearrange("o r c -> r o c").bitcast(I32),
+                )
+
+        xs = keep.tile([P, PASSES, T], U8, name="xs", align_bytes=64)
+        w1s = keep.tile([P, PASSES, H], U8, name="w1s", align_bytes=64)
+        w2s = keep.tile([P, PASSES, H], U8, name="w2s", align_bytes=64)
+        w3s = keep.tile([P, 1, N], U8, name="w3s", align_bytes=64)
+        nc.vector.memset(xs[:].bitcast(I32), 0)
+        nc.gpsimd.memset(w1s[:].bitcast(I32), 0)
+        nc.vector.memset(w2s[:].bitcast(I32), 0)
+        nc.vector.memset(w3s[:].bitcast(I32), 0)
+
+        offs_t = keep.tile([P, S // 16], U16, name="offs_t")
+        lft_t = keep.tile([P, S // 16], U16, name="lft_t")
+        rgt_t = keep.tile([P, S // 16], U16, name="rgt_t")
+        xw = [keep.tile([P, T], I32, name="xw%d" % o, align_bytes=64) for o in range(PASSES)]
+        w1 = keep.tile([P, PASSES, 2 * H], U8, name="w1", align_bytes=64)
+        w2 = keep.tile([P, PASSES, 2 * H], U8, name="w2", align_bytes=64)
+        w3 = keep.tile([P, 2 * N], U8, name="w3", align_bytes=64)
+        eps_t = keep.tile([P, TILES], F32, name="eps_t")
+        gain = keep.tile([P, H], F32, name="gain")
+
+        def load_words(o, cols):
+            nc.sync.dma_start(out=xw[o][:, cols], in_=x_words[o].rearrange("p n r -> p (n r)").bitcast(I32)[:, cols])
+
+        nc.sync.dma_start(offs_t[:], offs)
+        load_words(0, slice(0, T // 2))
+        load_planes(nc.sync, xs, x_scales)
+        load_planes(nc.gpsimd, w1s, w1_scales)
+        nc.sync.dma_start(lft_t[:], lft)
+        load_words(0, slice(T // 2, T))
+        load_words(1, slice(0, T))
+        nc.sync.dma_start(rgt_t[:], rgt)
+        nc.sync.dma_start(out=w1[:].bitcast(I32), in_=w1_words.rearrange("o p c -> p o c").bitcast(I32))
+        nc.sync.dma_start(out=w2[:].bitcast(I32), in_=w2_words.rearrange("o p c -> p o c").bitcast(I32))
+        load_planes(nc.sync, w2s, w2_scales)
+        with nc.allow_non_contiguous_dma(reason="one value a partition"):
+            nc.sync.dma_start(out=eps_t[:], in_=eps.rearrange("(t p) o -> p (t o)", p=P))
+        nc.sync.dma_start(out=gain[:], in_=unit.rearrange("h o -> o h").partition_broadcast(P))
+        nc.sync.dma_start(out=w3[:].bitcast(I32), in_=w3_words[0].bitcast(I32))
+        load_planes(nc.sync, w3s, w3_scales)
+
+        ident = keep.tile([P, P], F32, name="ident")
+        make_identity(nc, ident[:])
+        vb = [keep.tile([P, S + SPARE], F32, name="vb%d" % t) for t in range(TILES)]
+        vn5 = [keep.tile([P, S + SPARE], F32, name="vn5%d" % t) for t in range(TILES)]
+        for t in range(TILES):
+            nc.gpsimd.memset(vb[t][:, S:], 0.0)
+            nc.gpsimd.memset(vn5[t][:, S:], 0.0)
+
+        pw = [keep.tile([P, S], I32, name="pw%d" % o, align_bytes=64) for o in range(PASSES)]
+        ps = [keep.tile([P, S], U8, name="ps%d" % o, align_bytes=64) for o in range(PASSES)]
+        for o in range(PASSES):
+            nc.vector.tensor_copy(ps[o][:], xs[:, o, :].indirect(offs_t[:]))
+            nc.vector.tensor_copy(pw[o][:].bitcast(U32), xw[o][:].bitcast(U32).indirect(offs_t[:]))
+
+        def product(acc, w, ws, t):
+            for o in range(PASSES):
+                nc.tensor.matmul_mx(
+                    acc[:],
+                    lhsT=w[:, o, 2 * P * t : 2 * P * (t + 1)].bitcast(FP4X4),
+                    lhsT_scale=ws[:, o, P * t : P * (t + 1)],
+                    rhs=pw[o][:].bitcast(FP8X4),
+                    rhs_scale=ps[o][:],
+                    start=(o == 0),
+                    stop=(o == PASSES - 1),
+                )
+
+        hid = {}
+        last = TILES - 1
+        ww, sq, vl, vr, nb, rest, near, wn, vw, nr = {}, {}, {}, {}, {}, {}, {}, {}, {}, {}
+        whole = slice(0, S)
+
+        def front(t):
+            vv = psum.tile([P, S], F32, name="vv", tag="vv")
+            ww[t] = psum.tile([P, S], F32, name="ww", tag="ww", bufs=3)
+            product(vv, w1, w1s, t)
+            product(ww[t], w2, w2s, t)
+            nc.scalar.activation(vb[t][:, :S], vv[:], ACT.Tanh)
+            for store, name in ((sq, "sq"), (vl, "vl"), (nb, "nb"), (rest, "rest"), (near, "near"), (wn, "wn"), (vw, "vw"), (nr, "nr")):
+                store[t] = work.tile([P, S], F32, name=name)
+            if t > 0:
+                nc.scalar.activation(sq[t][:], vb[t][:, :S], ACT.Square, scale=math.sqrt(0.24 / 1.4))
+            nc.scalar.activation(vl[t][:], vb[t][:].indirect(lft_t[:]), ACT.Copy)
+            if t not in FUSED:
+                vr[t] = work.tile([P, S], F32, name="vr")
+                nc.scalar.activation(vr[t][:], vb[t][:].indirect(rgt_t[:]), ACT.Copy)
+
+        def square(t, c):
+            nc.vector.scalar_tensor_tensor(sq[t][:, c], vb[t][:, c], 0.24 / 1.4, vb[t][:, c], ALU.mult, ALU.mult)
+
+        def cubic(t, c):
+            nc.vector.scalar_tensor_tensor(nb[t][:, c], sq[t][:, c], 1.0 / 1.4, vb[t][:, c], ALU.subtract, ALU.mult)
+
+        def local(t, c):
+            nc.vector.scalar_tensor_tensor(rest[t][:, c], ww[t][:, c], -0.4 / 1.4, nb[t][:, c], ALU.mult, ALU.subtract)
+
+        def neighbours(t, c):
+            if t in FUSED:
+                nc.vector.tensor_tensor(near[t][:, c], vb[t][:].indirect(rgt_t[:, c.start // 16 : c.stop // 16]), vl[t][:, c], ALU.add)
+            else:
+                nc.vector.tensor_tensor(near[t][:, c], vr[t][:, c], vl[t][:, c], ALU.add)
+
+        def voltage(t, c):
+            nc.vector.scalar_tensor_tensor(vn5[t][:, c], near[t][:, c], 0.2 / 1.4, rest[t][:, c], ALU.mult, ALU.add)
+
+        def recovery(t, c):
+            nc.vector.scalar_tensor_tensor(wn[t][:, c], vn5[t][:, c], eps_t[:, t : t + 1], ww[t][:, c], ALU.mult, ALU.add)
+
+        def coupling(t, c):
+            nc.vector.scalar_tensor_tensor(vw[t][:, c], wn[t][:, c], 0.7 * 1.4, vn5[t][:, c], ALU.mult, ALU.mult)
+
+        def fetch_right(t, c):
+            nc.scalar.activation(nr[t][:, c], vn5[t][:].indirect(rgt_t[:, c.start // 16 : c.stop // 16]), ACT.Copy, scale=1.4)
+
+        total = [psum.tile([P, H], F32, name="total%d" % b) for b in range(BLOCKS)]
+
+        def turn(t, blocks):
+            for b in blocks:
+                cols = slice(b * P, (b + 1) * P)
+                into = total[b][:, t * P : (t + 1) * P]
+                nc.tensor.matmul(into, vw[t][:, cols], ident[:], start=(t == 0), stop=False, is_transpose=True)
+                nc.tensor.matmul(into, nr[t][:, cols], ident[:], start=False, stop=(t == last), is_transpose=True)
+
+        def hidden(b):
+            hid[b] = work.tile([P, H], BF16, name="hid", align_bytes=64)
+            nc.vector.tensor_tensor(hid[b][:], total[b][:], gain[:], ALU.mult)
+
+        def read_out(b):
+            back = psum.tile([P, 2, P], F32, name="back", tag="ww", bufs=3)
+            pairs = hid[b][:].bitcast(F32)
+            for u in range(2):
+                nc.tensor.transpose(back[:, u, :], pairs[:, u::2], ident[:])
+            grouped = work.tile([P, P, 2], F32, name="grouped", align_bytes=64)
+            nc.scalar.copy(grouped[:], back[:].rearrange("p u j -> p j u"))
+            codes = work.tile([P, P], U32, name="codes", align_bytes=64)
+            plane = work.tile([P, P], U8, name="plane", align_bytes=64)
+            nc.vector.quantize_mx(
+                out=codes[:].bitcast(FP8X4), scales=plane[:], in_=grouped[:].rearrange("p j u -> p (j u)").bitcast(BF16)
+            )
+            acc = psum.tile([P, P], F32, name="acc", tag="total%d" % b)
+            nc.tensor.matmul_mx(
+                acc[:], lhsT=w3[:].bitcast(FP4X4), lhsT_scale=w3s[:, 0, :], rhs=codes[:].bitcast(FP8X4), rhs_scale=plane[:],
+                start=True, stop=True,
+            )
+            res = work.tile([P, P], F32, name="res")
+            nc.scalar.copy(res[:], acc[:])
+            nc.sync.dma_start(out=out[:, b * P : (b + 1) * P], in_=res[:])
+
+        halves = (slice(0, HALF), slice(HALF, S))
+        front(0)
+        front(1)
+        for step in (square, cubic, neighbours, local, voltage):
+            for c in halves:
+                step(0, c)
+        for t in range(last):
+            if t + 2 < TILES:
+                front(t + 2)
+            cubic(t + 1, whole)
+            recovery(t, whole)
+            local(t + 1, whole)
+            neighbours(t + 1, whole)
+            coupling(t, whole)
+            voltage(t + 1, whole)
+        for t in range(last - 1):
+            fetch_right(t, whole)
+            turn(t, range(BLOCKS))
+        for step in (recovery, coupling):
+            for c in halves:
+                step(last, c)
+        for h, c in enumerate(halves):
+            for t in (last - 1, last):
+                fetch_right(t, c)
+                turn(t, (2 * h, 2 * h + 1))
+        hidden(0)
+        for b in range(BLOCKS):
+            if b + 1 < BLOCKS:
+                hidden(b + 1)
+            read_out(b)

@@ -24,7 +24,7 @@ TILES = H // P
 BLOCKS = S // P
 SPARE = 16
 HALF = S // 2
-FUSED = (0,)
+FUSED = (0, 2)
 
 
 def tile_picked_yfhnag_mul_p_kernel(
@@ -43,7 +43,7 @@ def tile_picked_yfhnag_mul_p_kernel(
                     in_=scales[:, 4 * q : 4 * q + 4, :].rearrange("o r c -> r o c").bitcast(I32),
                 )
 
-        xs = keep.tile([P, PASSES, T], U8, name="xs", align_bytes=64)
+        xs = keep.tile([P, T], U8, name="xs", align_bytes=64)
         w1s = keep.tile([P, PASSES, H], U8, name="w1s", align_bytes=64)
         w2s = keep.tile([P, PASSES, H], U8, name="w2s", align_bytes=64)
         w3s = keep.tile([P, 1, N], U8, name="w3s", align_bytes=64)
@@ -67,13 +67,16 @@ def tile_picked_yfhnag_mul_p_kernel(
 
         nc.sync.dma_start(offs_t[:], offs)
         load_words(0, slice(0, T // 2))
-        load_planes(nc.sync, xs, x_scales)
+        for q in range(4):
+            nc.sync.dma_start(out=xs[32 * q : 32 * q + 8, :].bitcast(I32), in_=x_scales[:, 4 * q : 4 * q + 4, :].bitcast(I32))
         load_planes(nc.gpsimd, w1s, w1_scales)
         nc.sync.dma_start(lft_t[:], lft)
         load_words(0, slice(T // 2, T))
         load_words(1, slice(0, T))
+        w1_rows = w1_words.rearrange("o p c -> p o c")
+        nc.sync.dma_start(out=w1[:, :, : 2 * P].bitcast(I32), in_=w1_rows[:, :, : 2 * P].bitcast(I32))
         nc.sync.dma_start(rgt_t[:], rgt)
-        nc.sync.dma_start(out=w1[:].bitcast(I32), in_=w1_words.rearrange("o p c -> p o c").bitcast(I32))
+        nc.sync.dma_start(out=w1[:, :, 2 * P :].bitcast(I32), in_=w1_rows[:, :, 2 * P :].bitcast(I32))
         nc.sync.dma_start(out=w2[:].bitcast(I32), in_=w2_words.rearrange("o p c -> p o c").bitcast(I32))
         load_planes(nc.sync, w2s, w2_scales)
         with nc.allow_non_contiguous_dma(reason="one value a partition"):
@@ -87,38 +90,42 @@ def tile_picked_yfhnag_mul_p_kernel(
         vb = [keep.tile([P, S + SPARE], F32, name="vb%d" % t) for t in range(TILES)]
         vn5 = [keep.tile([P, S + SPARE], F32, name="vn5%d" % t) for t in range(TILES)]
         for t in range(TILES):
-            nc.gpsimd.memset(vb[t][:, S:], 0.0)
-            nc.gpsimd.memset(vn5[t][:, S:], 0.0)
+            nc.vector.memset(vb[t][:, S:], 0.0)
+            nc.vector.memset(vn5[t][:, S:], 0.0)
 
         pw = [keep.tile([P, S], I32, name="pw%d" % o, align_bytes=64) for o in range(PASSES)]
         ps = [keep.tile([P, S], U8, name="ps%d" % o, align_bytes=64) for o in range(PASSES)]
-        for o in range(PASSES):
-            nc.vector.tensor_copy(ps[o][:], xs[:, o, :].indirect(offs_t[:]))
-            nc.vector.tensor_copy(pw[o][:].bitcast(U32), xw[o][:].bitcast(U32).indirect(offs_t[:]))
+        nc.vector.memset(ps[1][:].bitcast(I32), 0)
+        nc.vector.tensor_copy(ps[0][:], xs[:].indirect(offs_t[:]))
+        for q in range(4):
+            nc.scalar.dma_start(out=ps[1][32 * q : 32 * q + 4, :].bitcast(I32), in_=ps[0][32 * q + 4 : 32 * q + 8, :].bitcast(I32))
+        whole = slice(0, S)
+        halves = (slice(0, HALF), slice(HALF, S))
+        for o, c in ((0, whole), (1, halves[0]), (1, halves[1])):
+            nc.vector.tensor_copy(pw[o][:, c].bitcast(U32), xw[o][:].bitcast(U32).indirect(offs_t[:, c.start // 16 : c.stop // 16]))
 
-        def product(acc, w, ws, t):
+        def product(acc, w, ws, t, c):
             for o in range(PASSES):
                 nc.tensor.matmul_mx(
                     acc[:],
                     lhsT=w[:, o, 2 * P * t : 2 * P * (t + 1)].bitcast(FP4X4),
                     lhsT_scale=ws[:, o, P * t : P * (t + 1)],
-                    rhs=pw[o][:].bitcast(FP8X4),
-                    rhs_scale=ps[o][:],
+                    rhs=pw[o][:, c].bitcast(FP8X4),
+                    rhs_scale=ps[o][:, c],
                     start=(o == 0),
                     stop=(o == PASSES - 1),
                 )
 
-        hid = {}
         last = TILES - 1
         ww, sq, vl, vr, nb, rest, near, wn, vw, nr = {}, {}, {}, {}, {}, {}, {}, {}, {}, {}
-        whole = slice(0, S)
 
         def front(t):
-            vv = psum.tile([P, S], F32, name="vv", tag="vv")
+            for c, bank in ((halves[0], "vv"), (halves[1], "total11")) if t == 0 else ((whole, "vv"),):
+                vv = psum.tile([P, c.stop - c.start], F32, name="vv", tag=bank)
+                product(vv, w1, w1s, t, c)
+                nc.scalar.activation(vb[t][:, c], vv[:], ACT.Tanh)
             ww[t] = psum.tile([P, S], F32, name="ww", tag="ww", bufs=3)
-            product(vv, w1, w1s, t)
-            product(ww[t], w2, w2s, t)
-            nc.scalar.activation(vb[t][:, :S], vv[:], ACT.Tanh)
+            product(ww[t], w2, w2s, t, whole)
             for store, name in ((sq, "sq"), (vl, "vl"), (nb, "nb"), (rest, "rest"), (near, "near"), (wn, "wn"), (vw, "vw"), (nr, "nr")):
                 store[t] = work.tile([P, S], F32, name=name)
             if t > 0:
@@ -155,24 +162,34 @@ def tile_picked_yfhnag_mul_p_kernel(
         def fetch_right(t, c):
             nc.scalar.activation(nr[t][:, c], vn5[t][:].indirect(rgt_t[:, c.start // 16 : c.stop // 16]), ACT.Copy, scale=1.4)
 
-        total = [psum.tile([P, H], F32, name="total%d" % b) for b in range(BLOCKS)]
+        total = {}
+        hid = [keep.tile([P, 2, P, 2], BF16, name="hid%d" % b, align_bytes=64) for b in range(BLOCKS)]
 
         def turn(t, blocks):
-            for b in blocks:
-                cols = slice(b * P, (b + 1) * P)
-                into = total[b][:, t * P : (t + 1) * P]
-                nc.tensor.matmul(into, vw[t][:, cols], ident[:], start=(t == 0), stop=False, is_transpose=True)
-                nc.tensor.matmul(into, nr[t][:, cols], ident[:], start=False, stop=(t == last), is_transpose=True)
+            for h in sorted(set(b // 2 for b in blocks)):
+                if t % 2 == 0:
+                    total[t // 2, h] = psum.tile([P, 2, 2, P], F32, name="total%d%d" % (t // 2, h))
+                for term in (nr, vw):
+                    for b in (2 * h, 2 * h + 1):
+                        nc.tensor.matmul(
+                            total[t // 2, h][:, b % 2, t % 2, :], term[t][:, b * P : (b + 1) * P], ident[:],
+                            start=(t % 2 == 0 and b % 2 == 0 and term is nr),
+                            stop=(t % 2 == 1 and b % 2 == 1 and term is vw),
+                            is_transpose=True,
+                        )
 
-        def hidden(b):
-            hid[b] = work.tile([P, H], BF16, name="hid", align_bytes=64)
-            nc.vector.tensor_tensor(hid[b][:], total[b][:], gain[:], ALU.mult)
+        def hidden(g, b):
+            nc.vector.tensor_tensor(
+                hid[b][:, :, g * 64 : (g + 1) * 64, :],
+                total[g, b // 2][:, b % 2, :, :].rearrange("j t (p u e) -> j u (t p) e", u=2, e=2),
+                gain[:, g * HALF : (g + 1) * HALF].rearrange("j (p u e) -> j u p e", u=2, e=2),
+                ALU.mult,
+            )
 
         def read_out(b):
             back = psum.tile([P, 2, P], F32, name="back", tag="ww", bufs=3)
-            pairs = hid[b][:].bitcast(F32)
             for u in range(2):
-                nc.tensor.transpose(back[:, u, :], pairs[:, u::2], ident[:])
+                nc.tensor.transpose(back[:, u, :], hid[b][:, u, :, :].rearrange("j p e -> j (p e)").bitcast(F32), ident[:])
             grouped = work.tile([P, P, 2], F32, name="grouped", align_bytes=64)
             nc.scalar.copy(grouped[:], back[:].rearrange("p u j -> p j u"))
             codes = work.tile([P, P], U32, name="codes", align_bytes=64)
@@ -180,7 +197,7 @@ def tile_picked_yfhnag_mul_p_kernel(
             nc.vector.quantize_mx(
                 out=codes[:].bitcast(FP8X4), scales=plane[:], in_=grouped[:].rearrange("p j u -> p (j u)").bitcast(BF16)
             )
-            acc = psum.tile([P, P], F32, name="acc", tag="total%d" % b)
+            acc = psum.tile([P, P], F32, name="acc", tag="total%d%d" % (b % 2, b // 2))
             nc.tensor.matmul_mx(
                 acc[:], lhsT=w3[:].bitcast(FP4X4), lhsT_scale=w3s[:, 0, :], rhs=codes[:].bitcast(FP8X4), rhs_scale=plane[:],
                 start=True, stop=True,
@@ -189,10 +206,11 @@ def tile_picked_yfhnag_mul_p_kernel(
             nc.scalar.copy(res[:], acc[:])
             nc.sync.dma_start(out=out[:, b * P : (b + 1) * P], in_=res[:])
 
-        halves = (slice(0, HALF), slice(HALF, S))
         front(0)
+        for c in halves:
+            square(0, c)
         front(1)
-        for step in (square, cubic, neighbours, local, voltage):
+        for step in (cubic, neighbours, local, voltage):
             for c in halves:
                 step(0, c)
         for t in range(last):
@@ -204,18 +222,21 @@ def tile_picked_yfhnag_mul_p_kernel(
             neighbours(t + 1, whole)
             coupling(t, whole)
             voltage(t + 1, whole)
-        for t in range(last - 1):
+        for t in range(last):
             fetch_right(t, whole)
             turn(t, range(BLOCKS))
+        hidden(0, 0)
         for step in (recovery, coupling):
             for c in halves:
                 step(last, c)
         for h, c in enumerate(halves):
-            for t in (last - 1, last):
-                fetch_right(t, c)
-                turn(t, (2 * h, 2 * h + 1))
-        hidden(0)
+            fetch_right(last, c)
+            turn(last, (2 * h, 2 * h + 1))
+        hidden(0, 1)
         for b in range(BLOCKS):
-            if b + 1 < BLOCKS:
-                hidden(b + 1)
-            read_out(b)
+            hidden(1, b)
+            if b + 2 < BLOCKS:
+                hidden(0, b + 2)
+            if b > 0:
+                read_out(b - 1)
+        read_out(BLOCKS - 1)

@@ -186,16 +186,20 @@ def tile_picked_yfhnag_mul_p_kernel(
                 ALU.mult,
             )
 
-        def read_out(b):
+        grouped = {}
+
+        def turn_back(b):
             back = psum.tile([P, 2, P], F32, name="back", tag="ww", bufs=3)
             for u in range(2):
                 nc.tensor.transpose(back[:, u, :], hid[b][:, u, :, :].rearrange("j p e -> j (p e)").bitcast(F32), ident[:])
-            grouped = work.tile([P, P, 2], F32, name="grouped", align_bytes=64)
-            nc.scalar.copy(grouped[:], back[:].rearrange("p u j -> p j u"))
+            grouped[b] = work.tile([P, P, 2], F32, name="grouped", align_bytes=64)
+            nc.scalar.copy(grouped[b][:], back[:].rearrange("p u j -> p j u"))
+
+        def read_out(b):
             codes = work.tile([P, P], U32, name="codes", align_bytes=64)
             plane = work.tile([P, P], U8, name="plane", align_bytes=64)
             nc.vector.quantize_mx(
-                out=codes[:].bitcast(FP8X4), scales=plane[:], in_=grouped[:].rearrange("p j u -> p (j u)").bitcast(BF16)
+                out=codes[:].bitcast(FP8X4), scales=plane[:], in_=grouped[b][:].rearrange("p j u -> p (j u)").bitcast(BF16)
             )
             acc = psum.tile([P, P], F32, name="acc", tag="total%d%d" % (b % 2, b // 2))
             nc.tensor.matmul_mx(
@@ -237,6 +241,7 @@ def tile_picked_yfhnag_mul_p_kernel(
             hidden(1, b)
             if b + 2 < BLOCKS:
                 hidden(0, b + 2)
-            if b > 0:
-                read_out(b - 1)
-        read_out(BLOCKS - 1)
+        for b in range(BLOCKS):
+            turn_back(b)
+        for b in range(BLOCKS):
+            read_out(b)

import math
from contextlib import ExitStack

import concourse.mybir as mybir
from concourse.masks import make_identity

K, T, S, N, H = 1024, 2048, 512, 128, 512
FLOPS = 2 * K * H * S * 2 + 2 * H * N * S

F32 = mybir.dt.float32
BF16 = mybir.dt.bfloat16
I32 = mybir.dt.int32
U32 = mybir.dt.uint32
U16 = mybir.dt.uint16
U8 = mybir.dt.uint8
FP8X4 = mybir.dt.float8_e4m3fn_x4
FP4X4 = mybir.dt.float4_e2m1fn_x4
ACT = mybir.ActivationFunctionType
ALU = mybir.AluOpType

P = 128
PASSES = K // 512
TILES = H // P
BLOCKS = S // P
SPARE = 16
HALF = S // 2
FUSED = (0, 2)


def tile_picked_yfhnag_mul_p_kernel(
    tc, x_words, x_scales, w1_words, w1_scales, w2_words, w2_scales, eps, unit, w3_words, w3_scales, offs, lft, rgt, out
):
    nc = tc.nc
    with ExitStack() as ctx:
        keep = ctx.enter_context(tc.tile_pool(name="keep", bufs=1))
        work = ctx.enter_context(tc.tile_pool(name="work", bufs=4))
        psum = ctx.enter_context(tc.psum_pool(name="psum", bufs=1))

        def load_planes(queue, plane, scales):
            for q in range(4):
                queue.dma_start(
                    out=plane[32 * q : 32 * q + 4].bitcast(I32),
                    in_=scales[:, 4 * q : 4 * q + 4, :].rearrange("o r c -> r o c").bitcast(I32),
                )

        xs = keep.tile([P, T], U8, name="xs", align_bytes=64)
        w1s = keep.tile([P, PASSES, H], U8, name="w1s", align_bytes=64)
        w2s = keep.tile([P, PASSES, H], U8, name="w2s", align_bytes=64)
        w3s = keep.tile([P, 1, N], U8, name="w3s", align_bytes=64)
        nc.vector.memset(xs[:].bitcast(I32), 0)
        nc.gpsimd.memset(w1s[:].bitcast(I32), 0)
        nc.vector.memset(w2s[:].bitcast(I32), 0)
        nc.vector.memset(w3s[:].bitcast(I32), 0)

        offs_t = keep.tile([P, S // 16], U16, name="offs_t")
        lft_t = keep.tile([P, S // 16], U16, name="lft_t")
        rgt_t = keep.tile([P, S // 16], U16, name="rgt_t")
        xw = [keep.tile([P, T], I32, name="xw%d" % o, align_bytes=64) for o in range(PASSES)]
        w1 = keep.tile([P, PASSES, 2 * H], U8, name="w1", align_bytes=64)
        w2 = keep.tile([P, PASSES, 2 * H], U8, name="w2", align_bytes=64)
        w3 = keep.tile([P, 2 * N], U8, name="w3", align_bytes=64)
        eps_t = keep.tile([P, TILES], F32, name="eps_t")
        gain = keep.tile([P, H], F32, name="gain")

        def load_words(o, cols):
            nc.sync.dma_start(out=xw[o][:, cols], in_=x_words[o].rearrange("p n r -> p (n r)").bitcast(I32)[:, cols])

        nc.sync.dma_start(offs_t[:], offs)
        load_words(0, slice(0, T // 2))
        for q in range(4):
            nc.sync.dma_start(out=xs[32 * q : 32 * q + 8, :].bitcast(I32), in_=x_scales[:, 4 * q : 4 * q + 4, :].bitcast(I32))
        load_planes(nc.gpsimd, w1s, w1_scales)
        nc.sync.dma_start(lft_t[:], lft)
        load_words(0, slice(T // 2, T))
        load_words(1, slice(0, T))
        w1_rows = w1_words.rearrange("o p c -> p o c")
        nc.sync.dma_start(out=w1[:, :, : 2 * P].bitcast(I32), in_=w1_rows[:, :, : 2 * P].bitcast(I32))
        nc.sync.dma_start(rgt_t[:], rgt)
        nc.sync.dma_start(out=w1[:, :, 2 * P :].bitcast(I32), in_=w1_rows[:, :, 2 * P :].bitcast(I32))
        nc.sync.dma_start(out=w2[:].bitcast(I32), in_=w2_words.rearrange("o p c -> p o c").bitcast(I32))
        load_planes(nc.sync, w2s, w2_scales)
        with nc.allow_non_contiguous_dma(reason="one value a partition"):
            nc.sync.dma_start(out=eps_t[:], in_=eps.rearrange("(t p) o -> p (t o)", p=P))
        nc.sync.dma_start(out=gain[:], in_=unit.rearrange("h o -> o h").partition_broadcast(P))
        nc.sync.dma_start(out=w3[:].bitcast(I32), in_=w3_words[0].bitcast(I32))
        load_planes(nc.sync, w3s, w3_scales)

        ident = keep.tile([P, P], F32, name="ident")
        make_identity(nc, ident[:])
        vb = [keep.tile([P, S + SPARE], F32, name="vb%d" % t) for t in range(TILES)]
        vn5 = [keep.tile([P, S + SPARE], F32, name="vn5%d" % t) for t in range(TILES)]
        for t in range(TILES):
            nc.vector.memset(vb[t][:, S:], 0.0)
            nc.vector.memset(vn5[t][:, S:], 0.0)

        pw = [keep.tile([P, S], I32, name="pw%d" % o, align_bytes=64) for o in range(PASSES)]
        ps = [keep.tile([P, S], U8, name="ps%d" % o, align_bytes=64) for o in range(PASSES)]
        nc.vector.memset(ps[1][:].bitcast(I32), 0)
        nc.vector.tensor_copy(ps[0][:], xs[:].indirect(offs_t[:]))
        for q in range(4):
            nc.scalar.dma_start(out=ps[1][32 * q : 32 * q + 4, :].bitcast(I32), in_=ps[0][32 * q + 4 : 32 * q + 8, :].bitcast(I32))
        whole = slice(0, S)
        halves = (slice(0, HALF), slice(HALF, S))
        for o, c in ((0, whole), (1, halves[0]), (1, halves[1])):
            nc.vector.tensor_copy(pw[o][:, c].bitcast(U32), xw[o][:].bitcast(U32).indirect(offs_t[:, c.start // 16 : c.stop // 16]))

        def product(acc, w, ws, t, c):
            for o in range(PASSES):
                nc.tensor.matmul_mx(
                    acc[:],
                    lhsT=w[:, o, 2 * P * t : 2 * P * (t + 1)].bitcast(FP4X4),
                    lhsT_scale=ws[:, o, P * t : P * (t + 1)],
                    rhs=pw[o][:, c].bitcast(FP8X4),
                    rhs_scale=ps[o][:, c],
                    start=(o == 0),
                    stop=(o == PASSES - 1),
                )

        last = TILES - 1
        ww, sq, vl, vr, nb, rest, near, wn, vw, nr = {}, {}, {}, {}, {}, {}, {}, {}, {}, {}

        def front(t):
            for c, bank in ((halves[0], "vv"), (halves[1], "total11")) if t == 0 else ((whole, "vv"),):
                vv = psum.tile([P, c.stop - c.start], F32, name="vv", tag=bank)
                product(vv, w1, w1s, t, c)
                nc.scalar.activation(vb[t][:, c], vv[:], ACT.Tanh)
            ww[t] = psum.tile([P, S], F32, name="ww", tag="ww", bufs=3)
            product(ww[t], w2, w2s, t, whole)
            for store, name in ((sq, "sq"), (vl, "vl"), (nb, "nb"), (rest, "rest"), (near, "near"), (wn, "wn"), (vw, "vw"), (nr, "nr")):
                store[t] = work.tile([P, S], F32, name=name)
            if t > 0:
                nc.scalar.activation(sq[t][:], vb[t][:, :S], ACT.Square, scale=math.sqrt(0.24 / 1.4))
            nc.scalar.activation(vl[t][:], vb[t][:].indirect(lft_t[:]), ACT.Copy)
            if t not in FUSED:
                vr[t] = work.tile([P, S], F32, name="vr")
                nc.scalar.activation(vr[t][:], vb[t][:].indirect(rgt_t[:]), ACT.Copy)

        def square(t, c):
            nc.vector.scalar_tensor_tensor(sq[t][:, c], vb[t][:, c], 0.24 / 1.4, vb[t][:, c], ALU.mult, ALU.mult)

        def cubic(t, c):
            nc.vector.scalar_tensor_tensor(nb[t][:, c], sq[t][:, c], 1.0 / 1.4, vb[t][:, c], ALU.subtract, ALU.mult)

        def local(t, c):
            nc.vector.scalar_tensor_tensor(rest[t][:, c], ww[t][:, c], -0.4 / 1.4, nb[t][:, c], ALU.mult, ALU.subtract)

        def neighbours(t, c):
            if t in FUSED:
                nc.vector.tensor_tensor(near[t][:, c], vb[t][:].indirect(rgt_t[:, c.start // 16 : c.stop // 16]), vl[t][:, c], ALU.add)
            else:
                nc.vector.tensor_tensor(near[t][:, c], vr[t][:, c], vl[t][:, c], ALU.add)

        def voltage(t, c):
            nc.vector.scalar_tensor_tensor(vn5[t][:, c], near[t][:, c], 0.2 / 1.4, rest[t][:, c], ALU.mult, ALU.add)

        def recovery(t, c):
            nc.vector.scalar_tensor_tensor(wn[t][:, c], vn5[t][:, c], eps_t[:, t : t + 1], ww[t][:, c], ALU.mult, ALU.add)

        def coupling(t, c):
            nc.vector.scalar_tensor_tensor(vw[t][:, c], wn[t][:, c], 0.7 * 1.4, vn5[t][:, c], ALU.mult, ALU.mult)

        def fetch_right(t, c):
            nc.scalar.activation(nr[t][:, c], vn5[t][:].indirect(rgt_t[:, c.start // 16 : c.stop // 16]), ACT.Copy, scale=1.4)

        total = {}
        hid = [keep.tile([P, 2, P, 2], BF16, name="hid%d" % b, align_bytes=64) for b in range(BLOCKS)]

        def turn(t, blocks):
            for h in sorted(set(b // 2 for b in blocks)):
                if t % 2 == 0:
                    total[t // 2, h] = psum.tile([P, 2, 2, P], F32, name="total%d%d" % (t // 2, h))
                for term in (nr, vw):
                    for b in (2 * h, 2 * h + 1):
                        nc.tensor.matmul(
                            total[t // 2, h][:, b % 2, t % 2, :], term[t][:, b * P : (b + 1) * P], ident[:],
                            start=(t % 2 == 0 and b % 2 == 0 and term is nr),
                            stop=(t % 2 == 1 and b % 2 == 1 and term is vw),
                            is_transpose=True,
                        )

        def hidden(g, b):
            nc.vector.tensor_tensor(
                hid[b][:, :, g * 64 : (g + 1) * 64, :],
                total[g, b // 2][:, b % 2, :, :].rearrange("j t (p u e) -> j u (t p) e", u=2, e=2),
                gain[:, g * HALF : (g + 1) * HALF].rearrange("j (p u e) -> j u p e", u=2, e=2),
                ALU.mult,
            )

        grouped = {}

        def turn_back(b):
            back = psum.tile([P, 2, P], F32, name="back", tag="ww", bufs=3)
            for u in range(2):
                nc.tensor.transpose(back[:, u, :], hid[b][:, u, :, :].rearrange("j p e -> j (p e)").bitcast(F32), ident[:])
            grouped[b] = work.tile([P, P, 2], F32, name="grouped", align_bytes=64)
            nc.scalar.copy(grouped[b][:], back[:].rearrange("p u j -> p j u"))

        def read_out(b):
            codes = work.tile([P, P], U32, name="codes", align_bytes=64)
            plane = work.tile([P, P], U8, name="plane", align_bytes=64)
            nc.vector.quantize_mx(
                out=codes[:].bitcast(FP8X4), scales=plane[:], in_=grouped[b][:].rearrange("p j u -> p (j u)").bitcast(BF16)
            )
            acc = psum.tile([P, P], F32, name="acc", tag="total%d%d" % (b % 2, b // 2))
            nc.tensor.matmul_mx(
                acc[:], lhsT=w3[:].bitcast(FP4X4), lhsT_scale=w3s[:, 0, :], rhs=codes[:].bitcast(FP8X4), rhs_scale=plane[:],
                start=True, stop=True,
            )
            res = work.tile([P, P], F32, name="res")
            nc.scalar.copy(res[:], acc[:])
            nc.sync.dma_start(out=out[:, b * P : (b + 1) * P], in_=res[:])

        front(0)
        for c in halves:
            square(0, c)
        front(1)
        for step in (cubic, neighbours, local, voltage):
            for c in halves:
                step(0, c)
        for t in range(last):
            if t + 2 < TILES:
                front(t + 2)
            cubic(t + 1, whole)
            recovery(t, whole)
            local(t + 1, whole)
            neighbours(t + 1, whole)
            coupling(t, whole)
            voltage(t + 1, whole)
        for t in range(last):
            fetch_right(t, whole)
            turn(t, range(BLOCKS))
        hidden(0, 0)
        for step in (recovery, coupling):
            for c in halves:
                step(last, c)
        for h, c in enumerate(halves):
            fetch_right(last, c)
            turn(last, (2 * h, 2 * h + 1))
        hidden(0, 1)
        for b in range(BLOCKS):
            hidden(1, b)
            if b + 2 < BLOCKS:
                hidden(0, b + 2)
        for b in range(BLOCKS):
            turn_back(b)
        for b in range(BLOCKS):
            read_out(b)
